import numpy as np, ml_dtypes
CORES = [1,5,17,21,33,37,49,53]
N = 8
BF = ml_dtypes.bfloat16
W, M, TV, S, B = 2560, 256, 4, 3, 1
QN = W // 16
def parts(rng):
    X = rng.integers(0, 256, (N, 8, 16, W)); z = rng.integers(0, 256, (N, 8, 16, M))
    o = np.argsort(rng.random((8, W)), axis=1); A, H, Q = o[:, :8], o[:, 8:40], o[:, 40:40 + QN]; gi = np.arange(8)[None, :, None, None]
    e = rng.integers(0, W, (N, 8, 16, W)); l = rng.integers(0, W, (N, 8, 16, M))
    e = np.where(rng.random(e.shape) < 0.2, H[gi, rng.integers(0, 32, e.shape)], e)
    l[:, :, 0] = H[gi[..., 0], rng.integers(0, 32, (N, 8, M))]
    for q in range(N):
        for g in range(8):
            lanes = rng.permutation(16)[:8]; sub = e[q, g]; sub[lanes[:, None], Q[g][None, :]] = A[g][:, None]
    barred = rng.random((N, 8, M)) < 0.06; barred[:, :, 5] = True
    lb = Q[gi, rng.integers(0, QN, (N, 8, 16, M))]; lb[:, :, 0] = A[gi[..., 0], rng.integers(0, 8, (N, 8, M))]
    keep = (rng.random((N, 8, 1, M)) < 0.5) & (np.arange(16)[None, None, :, None] == rng.integers(1, 16, (N, 8, 1, M)))
    l = np.where(barred[:, :, None, :] & ~keep, lb, l)
    return X, e, l, z, rng.integers(800, 1501, (N, 8))
def pack(X, e, l, z, th):
    return {"xt": np.ascontiguousarray(X.reshape(N, 128, W)).astype(np.float32).astype(BF), "ex": np.ascontiguousarray(e.reshape(N, 128, W)).astype(np.int32),
            "l0": np.ascontiguousarray(l.reshape(N, 128, M)).astype(np.int32), "z0": np.ascontiguousarray(z.reshape(N, 128, M)).astype(np.float32).astype(BF),
            "th": np.ascontiguousarray(th.reshape(N, 8, 1)).astype(np.int32)}
def setup_inputs(rng):
    return pack(*parts(rng))
def setup_inputs_spread(rng):
    def skew(top, rows, n):
        return np.minimum((top * rng.random((N, 8, rows, n)) ** np.exp2(rng.integers(-3, 4, (N, 8, 1, n)))).astype(np.int64), top - 1)
    return pack(skew(256, 16, W), skew(W, 16, W), skew(W, 16, M), skew(256, 16, M), rng.integers(0, 4081, (N, 8)))
def setup_inputs_ends(rng):
    ends = np.array([0, W - 1])
    def bits(n):
        u = rng.random((N, 8, 1, n)); return np.where(u < 0.3, 0, np.where(u < 0.6, 255, 255 * rng.integers(0, 2, (N, 8, 16, n))))
    X = bits(W); z = bits(M); sw = (np.arange(N)[:, None, None] + np.arange(8)[None, :, None]) % 2
    X[..., 0] = 255 * sw; X[..., W - 1] = 255 * (1 - sw); z[..., M - 1] = 0; z[..., 0] = 255
    u = rng.random((N, 8, 1, W)); u[..., 0] *= 0.7; u[..., W - 1] *= 0.7
    e = np.where(u < 0.25, 0, np.where(u < 0.5, W - 1, np.where(u < 0.7, ends[rng.integers(0, 2, (N, 8, 16, W))], rng.integers(0, W, (N, 8, 16, W)))))
    l = np.where(rng.random((N, 8, 16, M)) < 0.7, ends[rng.integers(0, 2, (N, 8, 16, M))], rng.integers(0, W, (N, 8, 16, M)))
    l[:, :, [2, 7, 15], M - 1] = W - 1; l[:, :, 0, M - 1] = 0
    th = np.stack([rng.permutation(np.array([0, 4080] * 4)) for q in range(N)]); th[N - 1] = np.array([0, 4080] * 4)
    return pack(X, e, l, z, th)
def setup_inputs_corners(rng):
    X, e, l, z, th = parts(rng); v = [int(a) for a in rng.permutation(8)]; i = np.arange(M); c = np.arange(W)
    e[:, v[0]] = np.where(rng.random((N, 16, W)) < 0.5, c, e[:, v[0]])
    l[:, v[0]] = np.where(rng.random((N, 16, M)) < 0.4, l[:, v[0], :1], l[:, v[0]]); l[:, v[0], :, ::8] = l[:, v[0], :1, ::8].copy()
    th[:, v[0]] = 4080
    o = rng.permutation(W); A, full, free = o[:8], o[8:8 + W // 2], o[8 + W // 2:]
    for g in (v[1], v[2]):
        e[:, g] = rng.choice(free, (N, 16, W))
        for q in range(N):
            lanes = rng.permutation(16)[:8]; sub = e[q, g]; sub[lanes[:, None], full[None, :]] = A[:, None]
        l[:, g] = rng.choice(full, (N, 16, M)); l[:, g, 0] = rng.choice(A, (N, M))
    l[:, v[2], 1 + i % 15, i] = rng.choice(free, (N, M)); j = i[1::2]
    l[:, v[2], 1 + (j + 7) % 15, j] = rng.choice(free, (N, len(j)))
    th[:, v[1]] = rng.choice(np.array([1, 4079]), N)
    l[:, v[3], 1:] = rng.integers(0, W, (N, 1, M)); th[:, v[3]] = 0
    X[:, v[4]] = X[:, v[4], :, :4].copy()[:, :, rng.integers(0, 4, W)]
    tips = np.array([0, 1, W - 2, W - 1]); e[:, v[5]] = rng.choice(tips, (N, 16, W)); l[:, v[5]] = rng.choice(tips, (N, 16, M))
    l[:, v[6], 1:] = rng.choice(o[-3:], (N, 15, M)); th[:, v[6]] = 4080
    e[:, v[7]] = (c[None, :] + 1 + np.arange(16)[:, None]) % W; l[:, v[7]] = rng.integers(W - 20, W, (N, 16, M))
    return pack(X, e, l, z, th)
def setup_inputs_crowd(rng):
    X, e, l, z, th = parts(rng); X = np.minimum(np.maximum(X, 1), 254)
    sizes = rng.permutation(np.array([1, 2, 3, 16, 64, 256, W, W]))
    for g in range(8):
        pool = rng.permutation(W)[:int(sizes[g])]
        e[:, g] = rng.choice(pool, (N, 16, W)); l[:, g, 1:] = rng.choice(pool, (N, 15, M))
    th[::2] = 4080; th[1::2] = 0
    return pack(X, e, l, z, th)
def setup_inputs_lull(rng):
    X = np.zeros((N, 8, 16, W), np.int64); e = np.zeros((N, 8, 16, W), np.int64); l = rng.integers(0, W, (N, 8, 16, M)); z = rng.integers(107, 149, (N, 8, 16, M))
    for g in range(8):
        o = rng.permutation(W); bar, grey = int(o[0]), int(o[1]); dl, dh, bl, bh = [o[2 + j::4] for j in range(4)]
        dark = np.concatenate([dl, dh]); bright = np.concatenate([bl, bh]); low = np.concatenate([dl, bl]); high = np.concatenate([dh, bh, o[:2]])
        x = X[:, g]; s = e[:, g]; m = l[:, g]; v = z[:, g]
        x[:, :, dark] = rng.integers(60, 101, (N, 16, len(dark))); x[:, :, bright] = rng.integers(155, 196, (N, 16, len(bright)))
        x[:, :, bar] = 255 * rng.integers(0, 2, (N, 16)); x[:, :, grey] = rng.integers(107, 149, (N, 16))
        s[:, :, low] = rng.choice(dark, (N, 16, len(low))); s[:, :, high] = rng.choice(bright, (N, 16, len(high)))
        s[:, 1, high] = rng.choice(bl, (N, len(high))); s[:, 2, high] = rng.choice(bh, (N, len(high)))
        np.put_along_axis(s, rng.integers(3, 15, (N, 1, W)), bar, 1)
        m[:, 0] = bar; m[:, 1] = np.stack([rng.permutation(low)[:M] for q in range(N)]); m[:, 2] = rng.choice(high[:-2], (N, M))
        m[:, 3:, 3::16] = grey; m[:, 4:, 11::16] = grey
        v[:, :, 3::16] = x[:, :, grey][:, :, None]; v[:, :, 11::16] = x[:, :, grey][:, :, None]
    th = np.zeros((N, 8), np.int64); th[::2] = rng.integers(1310, 1361, th[::2].shape); th[::2, rng.permutation(8)[:3]] = 4080
    return pack(X, e, l, z, th)
def check_inputs(d):
    bad = []
    for k, lo, hi in (("xt", 0, 255), ("ex", 0, W - 1), ("l0", 0, W - 1), ("z0", 0, 255), ("th", 0, 4080)):
        v = np.asarray(d[k]).astype(np.float64)
        if not (np.min(v) >= lo and np.max(v) <= hi): bad.append("range of " + k)
        elif not np.all(v == np.floor(v)): bad.append("whole numbers of " + k)
    return bad
def pick(w, ix):
    return np.take_along_axis(w, ix.reshape(8, 1, -1), 2).reshape((8, 16) + ix.shape[1:])
def at(l, k):
    return np.take_along_axis(l, k[:, None, :], 1)[:, 0]
def reference(xt, ex, l0, z0, th):
    X = xt.astype(np.float32).astype(np.int32).reshape(N, 8, 16, W); R = ex.astype(np.int64).reshape(N, 8, 16, W)
    L = l0.astype(np.int64).reshape(N, 8, 16, M); Z = z0.astype(np.float32).astype(np.int32).reshape(N, 8, 16, M); limit = th.astype(np.int64).reshape(N, 8, 1)
    count = [0] * N; kk = np.arange(16)[None, :, None]; gg = np.arange(8)[:, None] + np.zeros((8, M), np.int64); ii = np.arange(M)[None, :] + np.zeros((8, M), np.int64)
    for t in range(TV):
        for h in range(N):
            q = (h + S * t) % N; x = X[q]; l = L[h].copy(); z = Z[h].copy()
            d = np.add.reduce(np.abs(pick(x, l) - z[:, :, None, :]), axis=1).astype(np.int64)
            conf = np.any(pick(R[q], l) == l[:, None, :1, :], axis=1)
            key = np.where(conf, 2 ** 16 + kk, 16 * d + kk); key[:, 0] = 2 ** 20
            o = np.argsort(key, axis=1, kind="stable"); ra = o[:, 0]; rb = o[:, 1]
            la = at(l, ra); lb = at(l, rb); e = []
            Ea = pick(R[q], la); Eb = pick(R[q], lb)
            for E in (Ea, Eb):
                de = np.add.reduce(np.abs(pick(x, E) - z[:, :, None, :]), axis=1)
                e.append(at(E, np.argmin(de, axis=1)))
            far = 16 * d + 15 - kk; far[:, 0] = -1
            np.put_along_axis(far, ra[:, None, :], -1, 1); np.put_along_axis(far, rb[:, None, :], -1, 1)
            new = l.copy()
            for v in e:
                p = np.argmax(far, axis=1); np.put_along_axis(far, p[:, None, :], -1, 1); np.put_along_axis(new, p[:, None, :], v[:, None, :], 1)
            xa = pick(x, e[0]); xb = pick(x, e[1])
            acc = np.add.reduce(np.abs(xa - xb), axis=1) < limit[q] + (count[h] & 63)
            new[:, 1:] = np.where(acc[:, None, :], Eb[:, 1:], new[:, 1:])
            first = np.full((8, W), M); np.minimum.at(first, (gg[acc], la[acc]), ii[acc])
            win = acc & (first[gg, la] == ii)
            R[q][gg[win], (ii[win] + t) & 15, la[win]] = l[:, 0][win]
            L[h] = new; Z[h] = (xa + xb) >> 1; count[h] = int(np.count_nonzero(acc))
    home = [(q - S * (TV - 1)) % N for q in range(N)]
    return {"yl": L[home].reshape(N, 128, M).astype(np.float32), "yz": Z[home].reshape(N, 128, M).astype(np.float32).astype(BF),
            "yr": np.add.reduce(R.reshape(N, 128, B, W // B), axis=2).astype(np.float32)}

import numpy as np
from concourse.bass import DstId, RemoteDMATransfer
from concourse.mybir import dt, AluOpType, AxisListType, ActivationFunctionType

OP = AluOpType
AF = ActivationFunctionType
W, M, HM, TV, STEP = 2560, 256, 128, 4, 3
BIG, FARK, CONF = 4194304.0, 1048576.0, 131072.0
CEN, TCEN = 1280.0, 2040.0
MAGIC = 12582912.0
GC = 1.5
CYC = 0.83
HOP = 80.0
HELP = 200.0
PIECES = 1
CUT = {(1, 1): 2, (0, 1): 2}
EARLY = {'reps_l01': 300, 'count': -1300, 'bits1': 9000, 'sel30': 6400, 'sel21': 100, 'far0': 23300, 'sel20': 6700, 'reps_l00': 100,
         'phase1x1': -300, 'far1': 400, 'limits': -8000, 'rvals0': -6000, 'phase20': -6000, 'phase21': -2000, 'reps_z0': -300,
         'phase1r1': 4000, 'sel31': 1900, 'rupd1': 1000, 'sel11': 3300, 'sel10': 9700, 'rupd0': 2000, 'reps_z1': -4600, 'phase1x0': 1000,
         'bits0': -3300, 'upd0': -300, 'rvals1': -3300, 'upd1': 300}
BYPE = ((0, 0),)

SCRATCH, BANK, ORDER = {}, {}, {}


WHAT, AT = {}, {}


def _buf(name, shape, dtype, where="sbuf"):
    WHAT[name] = (where, shape, dtype)
    if where == "psum" or len(shape) > 2 or shape[1] > 2048:
        SCRATCH[name] = WHAT[name]
        return
    host = "all_" + dtype
    at = SCRATCH[host][1][1] if host in SCRATCH else 0
    AT[name] = (host, at)
    SCRATCH[host] = ("sbuf", [128, at + -(-shape[1] // 64) * 64], dtype)


def _declare():
    B, F, H, I, U = "bfloat16", "float32", "float16", "int32", "uint16"
    sq = [128, 128]
    for n, s, d in (("XW", [128, W], B), ("RI", [128, W], I), ("RW", [128, W + M], F), ("LI", [128, M], I)):
        _buf(n, s, d)
    for t in range(TV):
        for n, d in (("LF", U), ("LC", H), ("ZB", B), ("LFo", U), ("LCo", H), ("ZBo", B), ("L0B", F)):
            _buf("%s%d" % (n, t), [128, M], d)
        _buf("CN%d" % t, [128, 1], F)
        _buf("CNo%d" % t, [128, 1], F)
    for h in range(2):
        for n, s, d in (("L0R", [128, 2048], F), ("ZR", [128, 2048], B), ("GX", [128, 2048], B), ("AD", [128, 2048], B), ("CF", [128, 2048], B),
                        ("DA", [128, 2048], B), ("DB", [128, 2048], B), ("KEY", sq, F), ("LOSE", sq, F), ("KF", sq, F), ("LS", sq, F),
                        ("M1", sq, F), ("M2", sq, F), ("MF", sq, F), ("MG", sq, F), ("KE", [128, 256], F), ("OAB", [128, 256], B),
                        ("OL", [128, 256], H), ("LOF", [128, 16], U), ("EU", [128, 256], U), ("EC", [128, 256], H), ("ME", [128, 256], F),
                        ("OE", [128, 256], B), ("OEE", [128, 256], H), ("LEF", [128, 16], U), ("XE", [128, 256], B), ("AE", sq, B),
                        ("ACT", sq, B), ("ACN", sq, B), ("FF", [128, 256], B), ("FN", [128, 256], B), ("UU", [128, 256], H),
                        ("KL", sq, H), ("TT", sq, F), ("BI", sq, I), ("WM", sq, B)):
            _buf("%s_%d" % (n, h), s, d)
    for n, s, d in (("FTe", [128, 256], B), ("FTo", [128, 256], B), ("EQ", [128, 3072], B), ("LAD", [128, 16], F), ("SCF", [128, 16], F),
                    ("SCG", [128, 16], F), ("SCU", [128, 16], U), ("EAM", [128, 256], F), ("L0S", [128, 256], F), ("THT", sq, F),
                    ("THN", sq, F), ("COLS", [128, 16], F), ("NI", [128, 1], I), ("LY", [128, 256], F), ("IA", sq, I), ("IB", sq, I),
                    ("IC", sq, I), ("ID", [128, 264], I), ("IP", [128, 16], I), ("IQ", [128, 16], I), ("IG", [8, 128], I), ("IE", [128, 1], I),
                    ("DELTA", sq, B), ("BOb", sq, B), ("BOh", sq, H), ("Ib", sq, B), ("NIb", sq, B), ("HIb", sq, B), ("Ih", sq, H),
                    ("NIh", sq, H), ("QB", sq, B), ("TRI", sq, B), ("NDEL", sq, B), ("ONb", sq, B), ("ONh", sq, H), ("SB", [128, 264], F),
                    ("NSB", [128, 264], F), ("SEL0", sq, H), ("BLK", [128, 16], B), ("BLKC", [128, 8], B), ("CK", [128, 256], B),
                    ("CKE", [128, 256], B), ("BC", [128, 16], U), ("CC", sq, F), ("RMIN", [128, 256], F), ("RMAX", sq, F),
                    ("SELA", [128, 16, 128], H), ("PW", [128, 16], F), ("PX", [128, 16], F), ("DUM", [128, 16], F), ("DMC", [128, 16], F),
                    ("GB8", [8, 128], H), ("THI", [8, 1], I), ("THF", [8, 1], F), ("THH", [8, 1], H), ("THG", [8, 128], H)):
        _buf(n, s, d)
    for n, s, k in (("P0", [128, 512], 0), ("P1", [128, 512], 1), ("PB_0", [128, 512], 2), ("PB_1", [128, 512], 3), ("P4", [128, 512], 4), ("P5", [128, 512], 5), ("P6", [128, 512], 6), ("P7", [128, 512], 7)):
        _buf(n, s, F, "psum")
        BANK[n] = k


_declare()
SEMAPHORES = ["sV", "sS", "sP", "sG", "snt"] + ["ld%d" % i for i in range(12)]
for _t in range(1, TV):
    SEMAPHORES += ["l0%d" % _t, "cn%d" % _t] + ["z%d_%d" % (_t, h) for h in range(2)] + ["l%d_%d" % (_t, h) for h in range(2)]
SCOL, CME, CCE, CMO, CCO, CP0, CNEG, CTH0, CTH, CNR, CM15 = range(11)


def rank_program(g, core, T, topo):
    rank = T.rank_of(core)
    if rank is None:
        return
    N = len(T.cores)
    V, S, P = g.vector, g.scalar, g.tensor
    ops, hist, ndma, stage = [], {}, [0], ["start"]
    full = slice(None)

    def v(name, *idx):
        where, shape, dtype = WHAT[name]
        sl = list(idx) + [full] * (len(shape) - len(idx))
        lo = hi = 0
        n, stride, lane = 1, 1, None
        for d in range(len(shape) - 1, 0, -1):
            a, b, st = sl[d].indices(shape[d]) if isinstance(sl[d], slice) else (sl[d], sl[d] + 1, 1)
            c = (b - a + st - 1) // st
            lo += a * stride
            hi += (a + (c - 1) * st) * stride
            n *= c
            if d == len(shape) - 1 and st == 16:
                lane = a % 16
            stride *= shape[d]
        if name in AT:
            host, at = AT[name]
            a, b, st = sl[1].indices(shape[1])
            p0, p1, _ = sl[0].indices(shape[0])
            ap = T[host][p0:p1, at + a:at + b:st]
        else:
            ap = T[name][tuple(sl)]
        return {"ap": ap, "name": name, "lo": lo, "hi": hi + 1, "lane": lane, "n": n,
                "psum": where == "psum", "two": dtype in ("bfloat16", "float16", "uint16")}

    def cols(name, lo, hi, st=1):
        return v(name, full, slice(lo, hi, st))

    def col(j):
        return cols("COLS", j, j + 1)

    def ind(win, off):
        return {"ap": win["ap"].indirect(off["ap"]), "parts": [win, off], "n": 16 * off["n"], "psum": False, "two": False, "ind": True}

    def flat(aps):
        out = []
        for a in aps:
            if isinstance(a, dict):
                out += a["parts"] if "parts" in a else [a]
        return out

    def hit(a, b):
        return a[5] == b[5] and a[2] < b[3] and b[2] < a[3] and (a[4] is None or b[4] is None or a[4] == b[4])

    def op(eng, cost, reads, writes, fns, **kw):
        i = len(ops)
        o = {"i": i, "eng": eng, "cost": cost, "stage": stage[0], "fns": fns, "deps": set(), "order": set(kw.pop("after", ()))}
        o.update(kw)
        for a, wr in [(a, 0) for a in flat(reads)] + [(a, 1) for a in flat(writes)]:
            key = BANK.get(a["name"], a["name"])
            me = (i, wr, a["lo"], a["hi"], a["lane"], a["name"])
            old = hist.setdefault(key, [])
            if a["psum"] and eng == "P":
                for e in old:
                    if e[0] != i:
                        o["order" if ops[e[0]]["eng"] == "P" else "deps"].add(e[0])
                hist[key] = [e for e in old if e[0] == i] + [me]
                continue
            keep = []
            for e in old:
                if e[0] != i:
                    if a["psum"] and ops[e[0]]["eng"] != eng:
                        o["deps"].add(e[0])
                    elif (wr or e[1]) and hit(me, e):
                        o["deps"].add(e[0])
                        if wr and a["lane"] is None and not a["psum"] and a["lo"] <= e[2] and e[3] <= a["hi"]:
                            continue
                keep.append(e)
            keep.append(me)
            hist[key] = keep
        ops.append(o)
        return i

    def cyc(n, half):
        return max(64, n * (0.5 if half else 1)) * CYC + 60

    def tt(out, a, b, o):
        if "ind" in out:
            c = 50 + out["n"] * 3.5 * CYC
        elif "ind" in a:
            c = 50 + a["n"] * GC * CYC
        else:
            c = cyc(a["n"], False) if (a["psum"] or b["psum"]) else cyc(2 * a["n"], False)
        return op("V", c, [a, b], [out], [lambda: V.tensor_tensor(out["ap"], a["ap"], b["ap"], o)])

    def ts(out, a, s1, o1, s2=None, o2=None):
        def f():
            x1 = s1["ap"] if isinstance(s1, dict) else s1
            x2 = s2["ap"] if isinstance(s2, dict) else s2
            if o2 is None:
                return V.tensor_scalar(out["ap"], a["ap"], x1, None, o1)
            return V.tensor_scalar(out["ap"], a["ap"], x1, x2, o1, o2)
        return op("V", cyc(a["n"], a["two"] and out["two"]), [a, s1, s2], [out], [f])

    def cp(out, a):
        c = 50 + a["n"] * GC * CYC if "ind" in a else cyc(a["n"], a["two"] and out["two"])
        return op("V", c, [a], [out], [lambda: V.tensor_copy(out["ap"], a["ap"])])

    def fill(out, x):
        return op("V", cyc(out["n"], out["two"]), [], [out], [lambda: V.memset(out["ap"], x)])

    def scan(out, d0, d1, o0, o1):
        return op("V", cyc(d0["n"], False), [d0, d1], [out], [lambda: V.tensor_tensor_scan(out["ap"], d0["ap"], d1["ap"], 0.0, o0, o1)])

    def total(out, a):
        return op("V", cyc(a["n"], False), [a], [out], [lambda: V.tensor_reduce(out["ap"], a["ap"], AxisListType.X, OP.add)])

    def act(out, a, f, **kw):
        c = (65 + a["n"] * GC * CYC) if "ind" in a else a["n"] * CYC + 100
        return op("S", c, [a] + list(kw.values()), [out],
                  [lambda: S.activation(out["ap"], a["ap"], f, **{k: (x["ap"] if isinstance(x, dict) else x) for k, x in kw.items()})])

    def either(out, a):
        k = "ind" in a
        cv = 50 + a["n"] * GC * CYC if k else cyc(a["n"], a["two"] and out["two"])
        cs = 65 + a["n"] * GC * CYC if k else a["n"] * CYC + 100
        return op("VS", cv, [a], [out], [lambda: S.activation(out["ap"], a["ap"], AF.Copy)], costs={"V": cv, "S": cs},
                  alt=[lambda: V.tensor_copy(out["ap"], a["ap"])])

    def pe(*mms):
        c = sum(max(64, m[2]["n"]) * CYC + 5 for m in mms)
        return op("P", c, [x for m in mms for x in (m[1], m[2])], [m[0] for m in mms],
                  [(lambda m=m: P.matmul(m[0]["ap"], m[1]["ap"], m[2]["ap"], m[3], m[4])) for m in mms])

    def iota(out, pat, base, cm, small=False):
        def f():
            if small:
                return g.iota(out["ap"], pat, base, cm, allow_small_or_imprecise_dtypes=True)
            return g.iota(out["ap"], pat, base, cm)
        return op("G", 130 + 2 * out["n"] * CYC, [], [out], [f])

    def dma(q, out, a, reads=(), writes=(), cost=2500):
        k = ndma[0]
        ndma[0] += 1
        f = {"Y": lambda: g.sync.dma_start(out, a), "S": lambda: S.dma_start(out, a),
             "G": lambda: g.dma_start(out, a, allow_slow_non_contiguous=True)}[q]
        return op(q, 60, list(reads), list(writes), [f], dmasem="ld%d" % k, lat=cost)

    def send(items, sem, dsts=None, cost=1200):
        dsts = dsts or [T.cores[(rank + STEP) % N]] * len(items)
        at, tr = 0, []
        for it, d in zip(items, dsts):
            tr.append((it, topo.addr(d), sum(1 << e for e in topo.engines(core, d)[at:at + it[2]])))
            at += it[2]

        def f():
            if len(tr) == 1:
                it, (rid, pid, _), mk = tr[0]
                g.remote_dma(it[1]["ap"], it[0]["ap"], T.sem[sem[0]], T.sem["snt"], pid, rid, mk)
            else:
                g.remote_dma_fused([RemoteDMATransfer(dst_ids=[DstId(rid=ad[0], pnc=ad[1])], dma_engine_mask=mk, remote_sem=T.sem[sem[j % len(sem)]],
                                                      src=it[0]["ap"], dst=it[1]["ap"]) for j, (it, ad, mk) in enumerate(tr)], local_sem=T.sem["snt"])
        s = op("G", cost, [it[0] for it in items], [], [f], remote=at)
        for j, sm in enumerate(sem):
            mine = [it for q, it in enumerate(items) if q % len(sem) == j]
            op("R", 0, [], [it[1] for it in mine], [], arr=(sm, sum(it[2] for it in mine)), after=[s], pre=2500)

    H = [slice(0, HM), slice(HM, M)]
    def load(q, name, src, cost=2500):
        dma(q, v(name)["ap"], T[src][:], writes=[v(name)], cost=cost)
    load("Y", "LI", "l0", 2200)
    load("Y", "XW", "xt", 4500)
    load("S", "ZB0", "z0")
    load("S", "RI", "ex", 8000)
    load("G", "THI", "th")

    one = slice(0, 1)
    iota(v("IC"), [[-1, 128]], 0, 1)
    iota(v("IB"), [[-16, 8], [0, 16]], 0, 1)
    iota(v("IA"), [[0, 8], [-1, 16]], 16, 1)
    iota(v("IG"), [[1, 128]], 0, -16)
    iota(v("CK", one, slice(0, 128)), [[0, 8], [1, 16]], 0, 0, True)
    iota(v("CK", one, slice(128, 256)), [[0, 8], [-1, 16]], 16, 0, True)
    iota(v("CC"), [[0, 8], [1, 16]], 65536, 0, True)
    iota(v("CKE", one), [[0, 16], [1, 16]], 0, 0, True)
    iota(v("IP"), [[0, 16]], 0, 1)
    iota(v("IQ"), [[16, 16]], W, 0)
    iota(v("ID"), [[-1, 264]], 512, 1)
    cp(v("LF0"), v("LI"))
    ts(v("LC0"), v("LI"), -CEN, OP.add)
    ts(v("Ib"), v("IC"), 0, OP.is_equal)
    ts(v("NIb"), v("IC"), 0, OP.is_equal, -1.0, OP.mult)
    ts(v("IA"), v("IA"), 15, OP.bitwise_and)
    ts(v("DELTA"), v("IA"), 0, OP.is_equal)
    ts(col(CP0), cols("IA", 0, 1), 0, OP.is_equal)
    ts(v("IB"), v("IB"), 4, OP.arith_shift_right)
    ts(v("BOb"), v("IB"), 0, OP.is_equal)
    ts(v("BOh"), v("IB"), 0, OP.is_equal)
    ts(v("SEL0"), v("BOh"), col(CP0), OP.mult)
    ts(cols("BLK", 0, 8), cols("BOb", 0, 128, 16), 16.0, OP.mult)
    ts(cols("BLK", 8, 16), cols("BOb", 0, 128, 16), 16.0, OP.mult)
    ts(v("BLKC"), cols("BOb", 0, 128, 16), CONF, OP.mult)
    fill(v("CK", one, slice(0, 128, 16)), FARK)
    fill(v("CK", one, slice(128, 256, 16)), 0.0)
    fill(cols("CC", 0, 128, 16), FARK)
    fill(v("ONb"), 1.0)
    fill(v("RMIN"), 0.0)
    fill(cols("RMIN", 0, 256, 16), BIG)
    fill(v("RMAX"), 1.0)
    fill(cols("RMAX", 0, 128, 16), 0.0)
    ts(v("BC"), v("IQ"), 15 - W, OP.add)
    for h in range(2):
        fill(cols("LOSE_%d" % h, 0, 1), BIG)
        fill(cols("LS_%d" % h, 0, 1), 0.0)
    cp(cols("RW", 0, W), v("RI"))
    ts(v("Ih"), v("IC"), 0, OP.is_equal)
    ts(v("NIh"), v("IC"), 0, OP.is_equal, -1.0, OP.mult)
    fill(v("SELA"), 0.0)
    for a in range(16):
        cp(v("SELA", full, a, slice(a, 128, 16)), cols("BOh", a, 128, 16))
    ts(v("HIb"), v("IC"), 0, OP.is_equal, 0.5, OP.mult)
    ts(v("NDEL"), v("IA"), 0, OP.not_equal)
    fill(v("QB"), -1.0 / 512)
    ts(v("TRI"), v("IC"), 0, OP.is_ge, -2.0, OP.mult)
    ts(v("ID"), v("ID"), 15, OP.bitwise_and)
    ts(v("SB"), v("ID"), 0, OP.is_equal)
    ts(v("NSB"), v("ID"), 0, OP.not_equal)
    for j in range(12):
        fill(cols("PW", j, j + 1), float(2 ** (11 - j)))
    fill(cols("PW", 12, 16), 0.0)
    tt(v("PX"), v("PW"), cols("DELTA", 0, 16), OP.mult)
    total(col(SCOL), v("PX"))
    ts(v("IE"), cols("IP", 0, 1), 4, OP.arith_shift_right, 1, OP.bitwise_and)
    ts(col(CME), v("IE"), 0, OP.is_equal, 1.0 / 1024, OP.mult)
    ts(col(CCE), v("IE"), 0, OP.is_equal, -1.0, OP.mult)
    ts(col(CMO), v("IE"), 1.0 / 1024, OP.mult)
    ts(col(CCO), v("IE"), -1.0, OP.mult)
    fill(col(CM15), -15.0)
    ts(v("IP"), v("IP"), 15, OP.bitwise_and)
    tt(v("DUM"), v("IP"), v("IQ"), OP.add)
    ts(v("DMC"), v("DUM"), -1.0, OP.mult, CEN, OP.add)
    ts(v("IG"), v("IG"), 4, OP.arith_shift_right)
    ts(v("GB8"), v("IG"), 0, OP.is_equal)
    ts(v("THF"), v("THI"), -TCEN, OP.add)
    ts(v("THH"), v("THI"), -TCEN, OP.add)
    ts(v("THG"), v("GB8"), v("THF"), OP.mult)
    fill(v("ONh", slice(0, 8)), 1.0)
    pe((cols("P7", 0, 128), v("ONh", slice(0, 8)), v("THG"), True, True))
    ts(v("THT"), cols("P7", 0, 128), TCEN, OP.add)
    pe((cols("P7", 128, 129), v("GB8"), v("THH"), True, True))
    ts(col(CNEG), col(CP0), -100000.0, OP.mult)
    ts(col(CTH0), cols("P7", 128, 129), TCEN, OP.add, col(CNEG), OP.add)
    pe((cols("P6", 0, 256), v("SEL0"), v("LC0"), True, True))
    act(v("L0B0"), cols("P6", 0, 256), AF.Copy, bias=CEN)
    send([(v("L0B0"), v("L0B%d" % t), 2) for t in range(1, TV)], ["l0%d" % t for t in range(1, TV)],
         [T.cores[(rank + STEP * t) % N] for t in range(1, TV)])

    def hc(name, h, lo=0, hi=None):
        if name == "PU":
            return cols("PB_%d" % h, 256 + lo, 256 + hi)
        return cols("%s_%d" % (name, h), lo, hi if hi else WHAT["%s_%d" % (name, h)][1][1])

    def last(name, h, n=128):
        return ind(hc(name, h), cols("BC", 0, n // 16))

    def reps_l0(t, h):
        for k in range(1 if t else 0, 16):
            either(cols("L0R_%d" % h, k, 2048, 16), v("L0B%d" % t, full, H[h]))

    def reps_z(t, h):
        for k in range(16):
            either(cols("ZR_%d" % h, k, 2048, 16), v("ZB%d" % t, full, H[h]))

    def far_off(t, h, off, o0, G, AD, k0):
        for q in range(PIECES):
            a, b = HM * q // PIECES, HM * (q + 1) // PIECES
            either(cols(G, 16 * a, 16 * b), ind(v("XW"), cols(off, o0 + a, o0 + b)))
        for c in range(4):
            ks = [k for k in range(4 * c, 4 * c + 4) if k >= k0]
            for k in ks:
                o = cols("P%d" % (c % 2), 128 * (k % 4), 128 * (k % 4) + 128)
                pe((o, v("Ib"), cols(G, k, 2048, 16), True, False), (o, v("NIb"), v("ZB%d" % t, full, H[h]), False, True))
            lo, hi = ks[0], ks[-1] + 1
            act(cols(AD, 128 * lo, 128 * hi), cols("P%d" % (c % 2), 128 * (lo % 4), 128 * (hi - 4 * c)), AF.Abs)

    def phase1x(t, h):
        AD, PB = "AD_%d" % h, "PB_%d" % h
        far_off(t, h, "LF%d" % t, HM * h, "GX_%d" % h, AD, 1)
        pe((cols(PB, 0, 256), v("ONb", one), v("CK", one), True, False))
        for k in range(1, 16):
            pe((cols(PB, k, 256, 16), cols(AD, 128 * k, 128 * k + 128), v("BLK"), False, False))

    def phase1r(t, h):
        tt(hc("CF", h), ind(cols("RW", 0, W), v("LF%d" % t, full, H[h])), hc("L0R", h), OP.is_equal)
        pe(*[(cols("PB_%d" % h, k, 128, 16), cols("CF_%d" % h, k, 2048, 16), v("BLKC"), False, k == 15) for k in range(1, 16)])

    def pp(h, lo, hi):
        return cols("P5" if h else "P6", lo, hi)

    def lists(h, src, out, extra=None):
        o = pp(h, 256, 272)
        pe(*[(o, v("SELA", full, a), cols(src, a, 256, 16), a == 0, a == 15) for a in range(16)])
        ts(v(out), o, CEN, OP.add)
        if extra:
            tt(cols("LAD", 8 * h, 8 * h + 8), pp(h, 256, 264), cols("DMC", 8 * h, 8 * h + 8), OP.add)

    def sel1(t, h):
        tt(hc("KEY", h), cols("PB_%d" % h, 0, 128), v("CC"), OP.min)
        scan(hc("M1", h), cols("RMIN", 0, 128), hc("KEY", h), OP.max, OP.min)
        tt(hc("LOSE", h, 1, 128), hc("KEY", h, 1, 128), hc("M1", h, 0, 127), OP.max)
        tt(hc("OAB", h, 0, 128), last("M1", h), hc("KEY", h), OP.is_equal)
        scan(hc("M2", h), cols("RMIN", 0, 128), hc("LOSE", h), OP.max, OP.min)
        tt(hc("OAB", h, 128, 256), last("M2", h), hc("KEY", h), OP.is_equal)
        for l in range(2):
            p = pp(h, 128 * l, 128 * l + 128)
            pe((p, hc("OAB", h, 128 * l, 128 * l + 128), v("Ib"), True, True))
            tt(hc("OL", h, 128 * l, 128 * l + 128), p, v("LC%d" % t, full, H[h]), OP.mult)
        lists(h, "OL_%d" % h, "LOF_%d" % h, True)
        cp(hc("EU", h), ind(cols("RW", 0, W), hc("LOF", h)))
        ts(hc("EC", h), hc("EU", h), -CEN, OP.add)
        tt(hc("KF", h), last("M2", h), hc("KEY", h), OP.is_lt)

    def far(t, h):
        tt(hc("KF", h), cols("PB_%d" % h, 128, 256), hc("KF", h), OP.mult)
        scan(hc("MF", h), v("RMAX"), hc("KF", h), OP.mult, OP.max)
        tt(hc("LS", h, 1, 128), hc("KF", h, 1, 128), hc("MF", h, 0, 127), OP.min)
        tt(hc("FF", h, 0, 128), last("MF", h), hc("KF", h), OP.is_equal)
        scan(hc("MG", h), v("RMAX"), hc("LS", h), OP.mult, OP.max)
        tt(hc("FF", h, 128, 256), last("MG", h), hc("KF", h), OP.is_equal)
        f = [hc("FF", h, 0, 128), hc("FF", h, 128, 256)]
        pe(*[(cols("P7", 128 * l, 128 * l + 128), f[l], v("Ib"), True, True) for l in range(2)])
        act(hc("FN", h), cols("P7", 0, 256), AF.Copy)
        keep = cols("P7", 256, 384)
        pe((keep, f[0], v("NIb"), True, False), (keep, f[1], v("NIb"), False, False), (keep, v("ONb", one), v("ONb", one), False, True))
        tt(hc("KL", h), keep, v("LC%d" % t, full, H[h]), OP.mult)

    def bits(t, h):
        p = cols("P7", 384, 512)
        pe((p, v("BOh"), hc("OL", h, 0, 128), True, True))
        BI = hc("BI", h)
        ts(BI, p, CEN, OP.add, col(SCOL), OP.mult)
        ts(BI, BI, 2048, OP.bitwise_and)
        ts(v("FTe", full, H[h]), BI, col(CME), OP.mult, col(CCE), OP.add)
        ts(v("FTo", full, H[h]), BI, col(CMO), OP.mult, col(CCO), OP.add)
        for q in range(4):
            mm, n = [], 0
            for F in ("FTe", "FTo"):
                for hp in range(h + 1):
                    o, ps = cols("P%d" % (q % 2), n, n + 128), slice(32 * q, 32 * q + 32)
                    if hp == h:
                        mm.append((o, v("Ib"), v("TRI"), True, False))
                    mm.append((o, v(F, ps, H[hp]), v(F, ps, H[h]), hp != h, True))
                    n += 128
            pe(*mm)
            c = 1024 * h + n * q
            act(cols("EQ", c, c + n), cols("P%d" % (q % 2), 0, n), AF.Relu, bias=col(CM15))

    def phase2(t, h):
        for l, D in enumerate(("DA", "DB")):
            e = hc("EU", h, 128 * l, 128 * l + 128)
            if (h, l) in BYPE:
                far_off(t, h, "EU_%d" % h, 128 * l, "GX_%d" % h, "%s_%d" % (D, h), 0)
            else:
                cut = CUT.get((h, l), 1)
                for q in range(cut):
                    a, b = HM * q // cut, HM * (q + 1) // cut
                    d = hc(D, h, 16 * a, 16 * b)
                    tt(d, ind(v("XW"), hc("EU", h, 128 * l + a, 128 * l + b)), hc("ZR", h, 16 * a, 16 * b), OP.subtract)
                    act(d, d, AF.Abs)
        pe((cols("P4", 0, 256), v("ONb", one), v("CKE", one), True, False))
        for l, D in enumerate(("DA", "DB")):
            D = "%s_%d" % (D, h)
            pe(*[(cols("P4", 128 * l + j, 128 * l + 128, 16), cols(D, 128 * j, 128 * j + 128) if (h, l) in BYPE else cols(D, j, 2048, 16),
                  cols("BLK", 0, 8), False, l == 1 and j == 15) for j in range(16)])

    def sel2(t, h):
        act(hc("KE", h), cols("P4", 0, 256), AF.Copy)
        scan(hc("ME", h), v("RMIN"), hc("KE", h), OP.max, OP.min)
        tt(hc("OE", h), last("ME", h, 256), hc("KE", h), OP.is_equal)

    def sel3(t, h):
        pe(*[(pp(h, 128 * l, 128 * l + 128), hc("OE", h, 128 * l, 128 * l + 128), v("Ib"), True, True) for l in range(2)])
        tt(hc("OEE", h), pp(h, 0, 256), hc("EC", h), OP.mult)
        lists(h, "OEE_%d" % h, "LEF_%d" % h)
        cp(hc("XE", h), ind(v("XW"), hc("LEF", h)))
        pe((pp(h, 0, 256), v("BOh"), hc("OEE", h), True, True))
        tt(hc("UU", h), pp(h, 0, 256), hc("FN", h), OP.mult)
        xa, xb = hc("XE", h, 0, 128), hc("XE", h, 128, 256)
        p0, p1 = hc("PU", h, 0, 128), hc("PU", h, 128, 256)
        pe((p0, v("Ib"), xa, True, False), (p0, v("NIb"), xb, False, True))
        act(hc("AE", h), p0, AF.Abs)
        pe((p0, v("BOb"), hc("AE", h), True, True))
        pe((p1, hc("AE", h), v("BOb"), True, True))

    def upd(t, h):
        p0, p1 = hc("PU", h, 0, 128), hc("PU", h, 128, 256)
        xa, xb = hc("XE", h, 0, 128), hc("XE", h, 128, 256)
        ts(hc("ACN", h), p0, col(CTH), OP.is_lt)
        u, w = pp(h, 0, 128), pp(h, 128, 256)
        ua, ub, kl = hc("UU", h, 0, 128), hc("UU", h, 128, 256), hc("KL", h)
        pe((u, v("Ih"), kl, True, False), (u, v("Ih"), ua, False, False), (u, v("Ih"), ub, False, True),
           (w, v("Ih"), hc("EC", h, 128, 256), True, False), (w, v("NIh"), kl, False, False), (w, v("NIh"), ua, False, False), (w, v("NIh"), ub, False, True))
        tt(hc("TT", h), w, hc("ACN", h), OP.mult)
        lc, lf = v("LCo%d" % t, full, H[h]), v("LFo%d" % t, full, H[h])
        tt(lc, u, hc("TT", h), OP.add)
        if t < TV - 1:
            ts(lf, lc, CEN, OP.add)
            send([(lf, v("LF%d" % (t + 1), full, H[h]), 4), (lc, v("LC%d" % (t + 1), full, H[h]), 4)], ["l%d_%d" % (t + 1, h)])
        else:
            ts(v("LY", full, H[h]), lc, CEN, OP.add)
        tt(hc("ACT", h), p1, v("THN"), OP.is_lt)
        p0 = hc("PU", h, 0, 128)
        pe((p0, v("HIb"), xa, True, False), (p0, v("HIb"), xb, False, False), (p0, v("QB"), v("ONb"), False, True))
        zo = v("ZBo%d" % t, full, H[h])
        ts(zo, p0, MAGIC, OP.add, -MAGIC, OP.add)
        if t < TV - 1:
            send([(zo, v("ZB%d" % (t + 1), full, H[h]), 8)], ["z%d_%d" % (t + 1, h)])

    def rvals(t, h):
        i0 = HM * h + t
        tt(v("EAM", full, H[h]), ind(cols("RW", 0, W), hc("LOF", h, 0, 8)), cols("NSB", i0, i0 + HM), OP.mult)
        tt(v("L0S", full, H[h]), v("L0B%d" % t, full, H[h]), cols("SB", i0, i0 + HM), OP.mult)

    def rupd(t, h):
        P_ = "P5" if h else "P7"
        eq = lambda gg, hp: 1024 * h + 128 * ((h + 1) * gg + hp)
        pe((cols(P_, 0, 128), v("Ib"), v("NDEL"), True, False),
           *[(cols(P_, 16 * gg, 16 * gg + 16), cols("EQ", eq(gg, hp), eq(gg, hp) + 128),
              hc("ACT", hp, 16 * gg, 16 * gg + 16), False, gg == 7 and hp == h) for gg in range(8) for hp in range(h + 1)])
        tt(hc("WM", h), hc("ACT", h), cols(P_, 0, 128), OP.is_gt)
        pe((cols(P_, 256, 264), hc("WM", h), cols("BOb", 0, 128, 16), True, True))
        c = slice(8 * h, 8 * h + 8)
        tt(v("SCF", full, c), cols(P_, 256, 264), v("LAD", full, c), OP.mult)
        tt(v("SCG", full, c), v("SCF", full, c), v("DUM", full, c), OP.add)
        cp(v("SCU", full, c), v("SCG", full, c))
        tt(ind(v("RW"), v("SCU", full, c)), v("EAM", full, H[h]), v("L0S", full, H[h]), OP.add)

    def count(t):
        p = cols("P7", 288, 296)
        pe(*[(p, v("ONb"), cols("ACT_%d" % h, 0, 128, 16), h == 0, h == 1) for h in range(2)])
        total(col(CNR), p)
        cp(v("NI"), col(CNR))
        ts(v("NI"), v("NI"), 63, OP.bitwise_and)
        cp(v("CNo%d" % t), v("NI"))
        send([(v("CNo%d" % t), v("CN%d" % (t + 1)), 1)], ["cn%d" % (t + 1)])

    def do(part, name, t, h):
        stage[0] = name + str(h)
        part(t, h)

    for h in range(2):
        do(reps_l0, "reps_l0", 0, h)
    for t in range(TV):
        for h in range(2):
            do(phase1x, "phase1x", t, h)
        for h in range(2):
            do(phase1r, "phase1r", t, h)
            if t + 1 < TV:
                do(reps_l0, "reps_l0", t + 1, h)
        for h in range(2):
            do(reps_z, "reps_z", t, h)
            do(sel1, "sel1", t, h)
            if h:
                do(sel2, "sel2", t, 0)
            do(phase2, "phase2", t, h)
            do(far, "far", t, h)
            do(bits, "bits", t, h)
            do(rvals, "rvals", t, h)
        do(sel2, "sel2", t, 1)
        stage[0] = "limits"
        if t:
            ts(v("THN"), v("THT"), v("CN%d" % t), OP.add)
            ts(col(CTH), col(CTH0), v("CN%d" % t), OP.add)
        else:
            cp(v("THN"), v("THT"))
            cp(col(CTH), col(CTH0))
        for h in range(2):
            do(sel3, "sel3", t, h)
            do(upd, "upd", t, h)
            do(rupd, "rupd", t, h)
        if t + 1 < TV:
            stage[0] = "count"
            count(t)
        else:
            dma("Y", T["yl"][:], v("LY")["ap"], reads=[v("LY")])
            dma("Y", T["yz"][:], v("ZBo%d" % t)["ap"], reads=[v("ZBo%d" % t)])
    dma("Y", T["yr"][:], T["RW"][:, 0:W], reads=[cols("RW", 0, W)])

    n = len(ops)
    if "order" not in ORDER:
        succ, need, tail, ready = [[] for _ in range(n)], [0] * n, [0.0] * n, [0.0] * n
        for o in ops:
            pre = o["deps"] | o["order"]
            need[o["i"]] = len(pre)
            for d in pre:
                succ[d].append(o["i"])
        for i in range(n - 1, -1, -1):
            o = ops[i]
            tail[i] = o["cost"] + o.get("lat", 0) + o.get("pre", 0) + HOP + max([tail[j] for j in succ[i]] + [0.0])
        pri = [tail[o["i"]] + EARLY.get(o["stage"], 0) for o in ops]
        avail = {e: [] for o in ops for e in o["eng"]}
        free = {e: 0.0 for e in avail}

        def put(i):
            for e in ops[i]["eng"]:
                avail[e].append(i)
        for o in ops:
            if not need[o["i"]]:
                put(o["i"])
        order, plan, who = [], [], {}
        while len(order) < n:
            best = None
            for e, lst in avail.items():
                if e == "V":
                    lst = [j for j in lst if "costs" not in ops[j] or free["S"] > max(ready[j], free["V"]) + HELP]
                if lst:
                    first = min(ready[j] for j in lst)
                    est = first if e == "R" else max(free[e], first)
                    if best is None or est < best[0]:
                        best = (est, e, lst)
            est, e, lst = best
            i = max((j for j in lst if ready[j] <= est), key=lambda j: ("costs" not in ops[j] or e != "V", pri[j], -j))
            order.append(i)
            o = ops[i]
            for x in o["eng"]:
                avail[x].remove(i)
            who[i] = e
            fin = est + (o["costs"][e] if "costs" in o else o["cost"]) + o.get("pre", 0)
            if e != "R":
                free[e] = fin
            plan.append((est, fin, e, i))
            for j in succ[i]:
                ready[j] = max(ready[j], fin + o.get("lat", 0) + (HOP if i in ops[j]["deps"] or e == "R" else 0.0))
                need[j] -= 1
                if not need[j]:
                    put(j)
        ORDER["order"], ORDER["plan"], ORDER["who"], ORDER["ops"] = order, plan, who, ops
    order, who = ORDER["order"], ORDER["who"]

    que = {"V": V, "S": S, "P": P, "G": g, "Y": g.sync}
    count_, known, clock, place = {}, {}, {}, {}
    sent = 0
    for pos, i in enumerate(order):
        o = ops[i]
        e = who[i]
        if o["eng"] == "VS" and e == "V":
            o["fns"] = o["alt"]
        place[i] = pos
        if e == "R":
            clock[i] = (o["arr"][0], o["arr"][1], {})
            count_[o["arr"][0]] = o["arr"][1]
            continue
        kn = known.setdefault(e, {})
        for d in sorted(o["deps"], key=lambda j: -place[j]):
            sem, val, snap = clock[d]
            if kn.get(sem, 0) >= val:
                continue
            que[e].wait_ge(T.sem[sem], val)
            kn[sem] = val
            for s, x in snap.items():
                kn[s] = max(kn.get(s, 0), x)
        if "remote" in o:
            o["fns"][0]()
            sent += o["remote"]
        elif "dmasem" in o:
            o["fns"][0]().then_inc(T.sem[o["dmasem"]], 16)
            clock[i] = (o["dmasem"], 16, dict(kn))
            count_[o["dmasem"]] = 16
        else:
            s = "s" + e
            for f in o["fns"]:
                f().then_inc(T.sem[s], 1)
                count_[s] = count_.get(s, 0) + 1
            clock[i] = (s, count_[s], dict(kn))
    for s, x in count_.items():
        g.wait_ge(T.sem[s], x)
    g.wait_ge(T.sem["snt"], sent)
